import numpy as np
import ml_dtypes


def mxq(x, axis, fmt="e4m3"):
    dtype, down = {"e4m3": (ml_dtypes.float8_e4m3fn, 7), "e5m2": (ml_dtypes.float8_e5m2, 14)}[fmt]
    v = np.moveaxis(np.asarray(x, np.float32).astype(ml_dtypes.bfloat16).astype(np.float64), axis, -1)
    blocks = v.reshape(v.shape[:-1] + (-1, 32))
    amax = np.abs(blocks).max(-1, keepdims=True)
    byte = np.maximum(np.where(amax > 0, np.frexp(amax)[1] - 1 + 127, 0) - down, 1)
    scale = np.exp2(byte - 127.0)
    codes = (blocks / scale).astype(np.float32).astype(dtype).astype(np.float64)
    return np.moveaxis((codes * scale).reshape(v.shape), -1, axis)


WIDE = False


def mx_kscale(k, group=512):
    if not WIDE:
        return np.ones(k)
    levels = np.array([18, -18])
    if group != 512:
        return np.exp2(np.random.permutation(np.resize(levels, k // group))).repeat(group)
    if k % 512:
        return np.exp2(np.random.permutation(np.resize(levels, k // 32))).repeat(32)
    a = np.empty((k // 512, 16))
    for p in range(k // 512):
        a[p, :8] = np.random.permutation(np.resize(levels, 8))
        for g in range(8):
            far = levels[np.abs(levels - a[p, g]) >= 10]
            a[p, g + 8] = far[np.random.randint(len(far))]
    return np.exp2(a.ravel()).repeat(32)


def f64(x):
    return np.asarray(x).astype(np.float64)


E2M1 = np.array([0.0, 0.5, 1.0, 1.5, 2.0, 3.0, 4.0, 6.0, -0.0, -0.5, -1.0, -1.5, -2.0, -3.0, -4.0, -6.0])


def pack_group(w):
    k, n = w.shape
    w = f64(np.asarray(w, np.float32).astype(ml_dtypes.bfloat16)).reshape(k // 32, 32, n)
    amax = np.abs(w).max(1)
    mant, ex = np.frexp(amax / 6.0)
    byte = np.clip(np.where(amax > 0, np.where(mant > 0.5, ex, ex - 1) + 127, 1), 1, 254)
    scaled = (w * np.exp2(127.0 - byte)[:, None, :]).reshape(k, n).astype(np.float32)
    c = np.ascontiguousarray(scaled.reshape(k // 4, 4, n).transpose(0, 2, 1)).astype(ml_dtypes.float4_e2m1fn).view(np.uint8) & 0xF
    return np.ascontiguousarray((c[..., 0::2] | (c[..., 1::2] << 4)).reshape(k // 4, 2 * n)), byte.astype(np.uint8)


def unpack_group(words, scales):
    p, n = words.shape[0], scales.shape[1]
    words = np.ascontiguousarray(words).reshape(p, n, 2)
    nib = np.empty((p, n, 4), np.uint8)
    nib[..., 0::2] = words & 0xF
    nib[..., 1::2] = words >> 4
    return E2M1[nib].transpose(0, 2, 1).reshape(4 * p, n) * np.repeat(np.exp2(scales.astype(np.float64) - 127.0), 32, axis=0)


def gelu(v):
    return 0.5 * v * (1.0 + np.tanh(0.7978845608028654 * (v + 0.044715 * v ** 3)))


G, D, M, N = 4, 128, 256, 1024


def setup_inputs():
    n = np.random.standard_normal
    s = mx_kscale(D, 0)[:, None]
    w_ = [pack_group(w) for w in n((G, D, M)) / np.sqrt(D) / s]
    return {
        "x": (n((G, D, N)) * s).astype(np.float32),
        "w_words": np.stack([w[0] for w in w_]),
        "w_scales": np.stack([w[1] for w in w_]),
        "b": (0.5 * n((G, M, 1))).astype(np.float32),
        "r": n((G, M, N)).astype(np.float32),
    }


def reference(x, w_words, w_scales, b, r):
    xq = mxq(f64(x), 1, "e4m3")
    y = np.stack([unpack_group(w_words[g], w_scales[g]) for g in range(G)]).transpose(0, 2, 1) @ xq
    y = y + f64(b)
    y = gelu(y)
    y = y + f64(r)
    return y

@@ -1,0 +1,105 @@
+from contextlib import ExitStack
+
+import concourse.mybir as mybir
+
+G, D, M, N = 4, 128, 256, 1024
+FLOPS = 2 * G * D * M * N
+
+F32 = mybir.dt.float32
+BF16 = mybir.dt.bfloat16
+I32 = mybir.dt.int32
+U32 = mybir.dt.uint32
+U8 = mybir.dt.uint8
+FP8X4 = mybir.dt.float8_e4m3fn_x4
+FP4X4 = mybir.dt.float4_e2m1fn_x4
+GELU = mybir.ActivationFunctionType.Gelu_apprx_tanh
+ADD = mybir.AluOpType.add
+
+P = 128
+PACK = 4
+ROWS = D // PACK
+H = M // P
+CW = 512
+C = N // CW
+
+
+def tile_rows_glin_gelu_bias_res_kernel(tc, x, w_words, w_scales, b, r, out):
+    nc = tc.nc
+    with ExitStack() as ctx:
+        sb = ctx.enter_context(tc.tile_pool(name="sb", bufs=1))
+        ps = ctx.enter_context(tc.psum_pool(name="ps", bufs=1))
+        ctx.enter_context(tc.manual_schedule())
+
+        x_raw = sb.tile([P, PACK, N], F32, name="x_raw", align_bytes=64)
+        w_raw = sb.tile([P, 2 * M], U8, name="w_raw", align_bytes=64)
+        ws_raw = sb.tile([P, M], U8, name="ws_raw", align_bytes=64)
+        w_dealt = sb.tile([P, 2 * M], U8, name="w_dealt", align_bytes=64)
+        ws_dealt = sb.tile([P, M], U8, name="ws_dealt", align_bytes=64)
+        b_rows = sb.tile([P, M], F32, name="b_rows", align_bytes=64)
+        b_dealt = sb.tile([P, M], F32, name="b_dealt", align_bytes=64)
+        b_cols = sb.tile([P, M], F32, name="b_cols", align_bytes=64)
+        res = [sb.tile([P, H, N], F32, name="res%d" % g, align_bytes=64) for g in range(G)]
+        y = [sb.tile([P, H, N], F32, name="y%d" % g, align_bytes=64) for g in range(G)]
+        xb = [sb.tile([P, CW, PACK], BF16, name="xb%d" % c, align_bytes=64) for c in range(C)]
+        codes = [sb.tile([P, CW], U32, name="codes%d" % c, align_bytes=64) for c in range(C)]
+        xs = [sb.tile([P, CW], U8, name="xs%d" % c, align_bytes=64) for c in range(C)]
+        acc = [[ps.tile([P, CW], F32, name="acc%d_%d" % (g, h)) for h in range(H)] for g in range(G)]
+
+        nc.vector.memset(ws_raw[:].bitcast(I32), 0)
+        nc.vector.memset(b_rows[:], 0.0)
+
+        nc.sync.dma_start(out=x_raw[:], in_=x.rearrange("g (p j) n -> (g p) j n", j=PACK))
+        nc.scalar.dma_start(out=w_raw[:].bitcast(I32), in_=w_words.rearrange("g p c -> (g p) c").bitcast(I32))
+        for g in range(G):
+            nc.scalar.dma_start(out=ws_raw[ROWS * g : ROWS * g + 4, :].bitcast(I32), in_=w_scales[g].bitcast(I32))
+        nc.scalar.dma_start(
+            out=b_rows[0:P:32, :].rearrange("a (g k) -> a g k", g=G),
+            in_=b.rearrange("g (a k) o -> a g (k o)", a=4),
+        )
+        for g in range(G):
+            nc.sync.dma_start(out=res[g][:], in_=r[g].rearrange("(p h) n -> p h n", h=H))
+
+        nc.vector.tensor_copy(
+            out=w_dealt[:].rearrange("q (h p c) -> q h p c", h=H, c=2),
+            in_=w_raw[:].rearrange("q (p h c) -> q h p c", h=H, c=2),
+        )
+        nc.vector.tensor_copy(
+            out=ws_dealt[:].rearrange("q (h p) -> q h p", h=H),
+            in_=ws_raw[:].rearrange("q (p h) -> q h p", h=H),
+        )
+        nc.vector.tensor_copy(
+            out=b_dealt[:].rearrange("q (g h j) -> q g h j", g=G, h=H),
+            in_=b_rows[:].rearrange("q (g j h) -> q g h j", g=G, h=H),
+        )
+        nc.vector.transpose(out=b_cols[:], in_=b_dealt[:])
+
+        for c in range(C):
+            nc.vector.tensor_copy(
+                out=xb[c][:].rearrange("p (u i) j -> p u j i", i=4),
+                in_=x_raw[:, :, c * CW : (c + 1) * CW].rearrange("p j (u i) -> p u j i", i=4),
+            )
+            nc.vector.quantize_mx(
+                out=codes[c][:].bitcast(FP8X4),
+                scales=xs[c][:],
+                in_=xb[c][:].rearrange("p n j -> p (n j)"),
+            )
+
+        order = [(0, 0), (1, 0), (0, 1), (1, 1), (2, 0), (2, 1), (3, 0), (3, 1)]
+        for g, c in order:
+            rows = slice(ROWS * g, ROWS * (g + 1))
+            cols = slice(c * CW, (c + 1) * CW)
+            for h in range(H):
+                nc.tensor.matmul_mx(
+                    out=acc[g][h][:],
+                    lhsT=w_dealt[rows, 2 * P * h : 2 * P * (h + 1)].bitcast(FP4X4),
+                    lhsT_scale=ws_dealt[rows, P * h : P * (h + 1)],
+                    rhs=codes[c][rows, :].bitcast(FP8X4),
+                    rhs_scale=xs[c][rows, :],
+                    start=True,
+                    stop=True,
+                )
+                k = 32 * (H * g + h)
+                nc.scalar.activation(out=y[g][:, h, cols], in_=acc[g][h][:], func=GELU, bias=b_cols[:, k : k + 1])
+            nc.vector.tensor_tensor(out=y[g][:, :, cols], in0=y[g][:, :, cols], in1=res[g][:, :, cols], op=ADD)
+            if c == C - 1:
+                nc.sync.dma_start(out=out[g].rearrange("(p h) n -> p h n", h=H), in_=y[g][:])

@@ -21,6 +21,7 @@ ROWS = D // PACK
 H = M // P
 CW = 512
 C = N // CW
+SCALAR_COLS = (160, 320)
 
 
 def tile_rows_glin_gelu_bias_res_kernel(tc, x, w_words, w_scales, b, r, out):
@@ -38,6 +39,7 @@ def tile_rows_glin_gelu_bias_res_kernel(tc, x, w_words, w_scales, b, r, out):
         b_rows = sb.tile([P, M], F32, name="b_rows", align_bytes=64)
         b_dealt = sb.tile([P, M], F32, name="b_dealt", align_bytes=64)
         b_cols = sb.tile([P, M], F32, name="b_cols", align_bytes=64)
+        warm = sb.tile([P, 1], F32, name="warm", align_bytes=64)
         res = [sb.tile([P, H, N], F32, name="res%d" % g, align_bytes=64) for g in range(G)]
         y = [sb.tile([P, H, N], F32, name="y%d" % g, align_bytes=64) for g in range(G)]
         xb = [sb.tile([P, CW, PACK], BF16, name="xb%d" % c, align_bytes=64) for c in range(C)]
@@ -48,14 +50,16 @@ def tile_rows_glin_gelu_bias_res_kernel(tc, x, w_words, w_scales, b, r, out):
         nc.vector.memset(ws_raw[:].bitcast(I32), 0)
         nc.vector.memset(b_rows[:], 0.0)
 
+        nc.vector.memset(warm[:], 0.0)
         nc.sync.dma_start(out=x_raw[:], in_=x.rearrange("g (p j) n -> (g p) j n", j=PACK))
         nc.scalar.dma_start(out=w_raw[:].bitcast(I32), in_=w_words.rearrange("g p c -> (g p) c").bitcast(I32))
-        for g in range(G):
-            nc.scalar.dma_start(out=ws_raw[ROWS * g : ROWS * g + 4, :].bitcast(I32), in_=w_scales[g].bitcast(I32))
         nc.scalar.dma_start(
             out=b_rows[0:P:32, :].rearrange("a (g k) -> a g k", g=G),
             in_=b.rearrange("g (a k) o -> a g (k o)", a=4),
         )
+        nc.scalar.activation(out=warm[:], in_=warm[:], func=GELU)
+        for g in range(G):
+            nc.sync.dma_start(out=ws_raw[ROWS * g : ROWS * g + 4, :].bitcast(I32), in_=w_scales[g].bitcast(I32))
         for g in range(G):
             nc.sync.dma_start(out=res[g][:], in_=r[g].rearrange("(p h) n -> p h n", h=H))
 
@@ -64,42 +68,55 @@ def tile_rows_glin_gelu_bias_res_kernel(tc, x, w_words, w_scales, b, r, out):
             in_=w_raw[:].rearrange("q (p h c) -> q h p c", h=H, c=2),
         )
         nc.vector.tensor_copy(
-            out=ws_dealt[:].rearrange("q (h p) -> q h p", h=H),
-            in_=ws_raw[:].rearrange("q (p h) -> q h p", h=H),
-        )
-        nc.vector.tensor_copy(
             out=b_dealt[:].rearrange("q (g h j) -> q g h j", g=G, h=H),
             in_=b_rows[:].rearrange("q (g j h) -> q g h j", g=G, h=H),
         )
         nc.vector.transpose(out=b_cols[:], in_=b_dealt[:])
+        def interleave(copy, c, lo, hi):
+            copy(
+                out=xb[c][:, lo:hi, :].rearrange("p (u i) j -> p u j i", i=4),
+                in_=x_raw[:, :, c * CW + lo : c * CW + hi].rearrange("p j (u i) -> p u j i", i=4),
+            )
 
         for c in range(C):
-            nc.vector.tensor_copy(
-                out=xb[c][:].rearrange("p (u i) j -> p u j i", i=4),
-                in_=x_raw[:, :, c * CW : (c + 1) * CW].rearrange("p j (u i) -> p u j i", i=4),
-            )
+            interleave(nc.scalar.copy, c, 0, SCALAR_COLS[c])
+            interleave(nc.vector.tensor_copy, c, SCALAR_COLS[c], CW)
+            if c == 0:
+                nc.vector.tensor_copy(
+                    out=ws_dealt[:].rearrange("q (h p) -> q h p", h=H),
+                    in_=ws_raw[:].rearrange("q (p h) -> q h p", h=H),
+                )
             nc.vector.quantize_mx(
                 out=codes[c][:].bitcast(FP8X4),
                 scales=xs[c][:],
                 in_=xb[c][:].rearrange("p n j -> p (n j)"),
             )
 
-        order = [(0, 0), (1, 0), (0, 1), (1, 1), (2, 0), (2, 1), (3, 0), (3, 1)]
-        for g, c in order:
+        def product(g, h, c):
             rows = slice(ROWS * g, ROWS * (g + 1))
-            cols = slice(c * CW, (c + 1) * CW)
-            for h in range(H):
-                nc.tensor.matmul_mx(
-                    out=acc[g][h][:],
-                    lhsT=w_dealt[rows, 2 * P * h : 2 * P * (h + 1)].bitcast(FP4X4),
-                    lhsT_scale=ws_dealt[rows, P * h : P * (h + 1)],
-                    rhs=codes[c][rows, :].bitcast(FP8X4),
-                    rhs_scale=xs[c][rows, :],
-                    start=True,
-                    stop=True,
-                )
-                k = 32 * (H * g + h)
-                nc.scalar.activation(out=y[g][:, h, cols], in_=acc[g][h][:], func=GELU, bias=b_cols[:, k : k + 1])
-            nc.vector.tensor_tensor(out=y[g][:, :, cols], in0=y[g][:, :, cols], in1=res[g][:, :, cols], op=ADD)
-            if c == C - 1:
-                nc.sync.dma_start(out=out[g].rearrange("(p h) n -> p h n", h=H), in_=y[g][:])
+            nc.tensor.matmul_mx(
+                out=acc[g][h][:],
+                lhsT=w_dealt[rows, 2 * P * h : 2 * P * (h + 1)].bitcast(FP4X4),
+                lhsT_scale=ws_dealt[rows, P * h : P * (h + 1)],
+                rhs=codes[c][rows, :].bitcast(FP8X4),
+                rhs_scale=xs[c][rows, :],
+                start=True,
+                stop=True,
+            )
+            k = 32 * (H * g + h)
+            nc.scalar.activation(
+                out=y[g][:, h, c * CW : (c + 1) * CW], in_=acc[g][h][:], func=GELU, bias=b_cols[:, k : k + 1]
+            )
+
+        product(0, 0, 0)
+        for g in range(G):
+            product(g, 1, 0)
+            if g + 1 < G:
+                product(g + 1, 0, 0)
+            product(g, 0, 1)
+            product(g, 1, 1)
+            for c in range(C):
+                for h in range(H):
+                    part = y[g][:, h, c * CW : (c + 1) * CW]
+                    nc.vector.tensor_tensor(out=part, in0=part, in1=res[g][:, h, c * CW : (c + 1) * CW], op=ADD)
+            nc.sync.dma_start(out=out[g].rearrange("(p h) n -> p h n", h=H), in_=y[g][:])

@@ -21,7 +21,7 @@ ROWS = D // PACK
 H = M // P
 CW = 512
 C = N // CW
-SCALAR_COLS = (160, 320)
+SCALAR_COLS = (160, 256)
 
 
 def tile_rows_glin_gelu_bias_res_kernel(tc, x, w_words, w_scales, b, r, out):
@@ -115,8 +115,12 @@ def tile_rows_glin_gelu_bias_res_kernel(tc, x, w_words, w_scales, b, r, out):
                 product(g + 1, 0, 0)
             product(g, 0, 1)
             product(g, 1, 1)
+            out_rows = out[g].rearrange("(p h) n -> p h n", h=H)
             for c in range(C):
                 for h in range(H):
                     part = y[g][:, h, c * CW : (c + 1) * CW]
                     nc.vector.tensor_tensor(out=part, in0=part, in1=res[g][:, h, c * CW : (c + 1) * CW], op=ADD)
-            nc.sync.dma_start(out=out[g].rearrange("(p h) n -> p h n", h=H), in_=y[g][:])
+                    if g == G - 1 and c == C - 1:
+                        nc.sync.dma_start(out=out_rows[:, h, :], in_=y[g][:, h, :])
+            if g < G - 1:
+                nc.sync.dma_start(out=out_rows, in_=y[g][:])

from contextlib import ExitStack

import concourse.mybir as mybir

G, D, M, N = 4, 128, 256, 1024
FLOPS = 2 * G * D * M * N

F32 = mybir.dt.float32
BF16 = mybir.dt.bfloat16
I32 = mybir.dt.int32
U32 = mybir.dt.uint32
U8 = mybir.dt.uint8
FP8X4 = mybir.dt.float8_e4m3fn_x4
FP4X4 = mybir.dt.float4_e2m1fn_x4
GELU = mybir.ActivationFunctionType.Gelu_apprx_tanh
ADD = mybir.AluOpType.add

P = 128
PACK = 4
ROWS = D // PACK
H = M // P
CW = 512
C = N // CW
SCALAR_COLS = (160, 256)


def tile_rows_glin_gelu_bias_res_kernel(tc, x, w_words, w_scales, b, r, out):
    nc = tc.nc
    with ExitStack() as ctx:
        sb = ctx.enter_context(tc.tile_pool(name="sb", bufs=1))
        ps = ctx.enter_context(tc.psum_pool(name="ps", bufs=1))
        ctx.enter_context(tc.manual_schedule())

        x_raw = sb.tile([P, PACK, N], F32, name="x_raw", align_bytes=64)
        w_raw = sb.tile([P, 2 * M], U8, name="w_raw", align_bytes=64)
        ws_raw = sb.tile([P, M], U8, name="ws_raw", align_bytes=64)
        w_dealt = sb.tile([P, 2 * M], U8, name="w_dealt", align_bytes=64)
        ws_dealt = sb.tile([P, M], U8, name="ws_dealt", align_bytes=64)
        b_rows = sb.tile([P, M], F32, name="b_rows", align_bytes=64)
        b_dealt = sb.tile([P, M], F32, name="b_dealt", align_bytes=64)
        b_cols = sb.tile([P, M], F32, name="b_cols", align_bytes=64)
        warm = sb.tile([P, 1], F32, name="warm", align_bytes=64)
        res = [sb.tile([P, H, N], F32, name="res%d" % g, align_bytes=64) for g in range(G)]
        y = [sb.tile([P, H, N], F32, name="y%d" % g, align_bytes=64) for g in range(G)]
        xb = [sb.tile([P, CW, PACK], BF16, name="xb%d" % c, align_bytes=64) for c in range(C)]
        codes = [sb.tile([P, CW], U32, name="codes%d" % c, align_bytes=64) for c in range(C)]
        xs = [sb.tile([P, CW], U8, name="xs%d" % c, align_bytes=64) for c in range(C)]
        acc = [[ps.tile([P, CW], F32, name="acc%d_%d" % (g, h)) for h in range(H)] for g in range(G)]

        nc.vector.memset(ws_raw[:].bitcast(I32), 0)
        nc.vector.memset(b_rows[:], 0.0)

        nc.vector.memset(warm[:], 0.0)
        nc.sync.dma_start(out=x_raw[:], in_=x.rearrange("g (p j) n -> (g p) j n", j=PACK))
        nc.scalar.dma_start(out=w_raw[:].bitcast(I32), in_=w_words.rearrange("g p c -> (g p) c").bitcast(I32))
        nc.scalar.dma_start(
            out=b_rows[0:P:32, :].rearrange("a (g k) -> a g k", g=G),
            in_=b.rearrange("g (a k) o -> a g (k o)", a=4),
        )
        nc.scalar.activation(out=warm[:], in_=warm[:], func=GELU)
        for g in range(G):
            nc.sync.dma_start(out=ws_raw[ROWS * g : ROWS * g + 4, :].bitcast(I32), in_=w_scales[g].bitcast(I32))
        for g in range(G):
            nc.sync.dma_start(out=res[g][:], in_=r[g].rearrange("(p h) n -> p h n", h=H))

        nc.vector.tensor_copy(
            out=w_dealt[:].rearrange("q (h p c) -> q h p c", h=H, c=2),
            in_=w_raw[:].rearrange("q (p h c) -> q h p c", h=H, c=2),
        )
        nc.vector.tensor_copy(
            out=b_dealt[:].rearrange("q (g h j) -> q g h j", g=G, h=H),
            in_=b_rows[:].rearrange("q (g j h) -> q g h j", g=G, h=H),
        )
        nc.vector.transpose(out=b_cols[:], in_=b_dealt[:])
        def interleave(copy, c, lo, hi):
            copy(
                out=xb[c][:, lo:hi, :].rearrange("p (u i) j -> p u j i", i=4),
                in_=x_raw[:, :, c * CW + lo : c * CW + hi].rearrange("p j (u i) -> p u j i", i=4),
            )

        for c in range(C):
            interleave(nc.scalar.copy, c, 0, SCALAR_COLS[c])
            interleave(nc.vector.tensor_copy, c, SCALAR_COLS[c], CW)
            if c == 0:
                nc.vector.tensor_copy(
                    out=ws_dealt[:].rearrange("q (h p) -> q h p", h=H),
                    in_=ws_raw[:].rearrange("q (p h) -> q h p", h=H),
                )
            nc.vector.quantize_mx(
                out=codes[c][:].bitcast(FP8X4),
                scales=xs[c][:],
                in_=xb[c][:].rearrange("p n j -> p (n j)"),
            )

        def product(g, h, c):
            rows = slice(ROWS * g, ROWS * (g + 1))
            nc.tensor.matmul_mx(
                out=acc[g][h][:],
                lhsT=w_dealt[rows, 2 * P * h : 2 * P * (h + 1)].bitcast(FP4X4),
                lhsT_scale=ws_dealt[rows, P * h : P * (h + 1)],
                rhs=codes[c][rows, :].bitcast(FP8X4),
                rhs_scale=xs[c][rows, :],
                start=True,
                stop=True,
            )
            k = 32 * (H * g + h)
            nc.scalar.activation(
                out=y[g][:, h, c * CW : (c + 1) * CW], in_=acc[g][h][:], func=GELU, bias=b_cols[:, k : k + 1]
            )

        product(0, 0, 0)
        for g in range(G):
            product(g, 1, 0)
            if g + 1 < G:
                product(g + 1, 0, 0)
            product(g, 0, 1)
            product(g, 1, 1)
            out_rows = out[g].rearrange("(p h) n -> p h n", h=H)
            for c in range(C):
                for h in range(H):
                    part = y[g][:, h, c * CW : (c + 1) * CW]
                    nc.vector.tensor_tensor(out=part, in0=part, in1=res[g][:, h, c * CW : (c + 1) * CW], op=ADD)
                    if g == G - 1 and c == C - 1:
                        nc.sync.dma_start(out=out_rows[:, h, :], in_=y[g][:, h, :])
            if g < G - 1:
                nc.sync.dma_start(out=out_rows, in_=y[g][:])
